import numpy as np
import ml_dtypes


def mxq(x, axis, fmt="e4m3"):
    dtype, down = {"e4m3": (ml_dtypes.float8_e4m3fn, 7), "e5m2": (ml_dtypes.float8_e5m2, 14)}[fmt]
    v = np.moveaxis(np.asarray(x, np.float32).astype(ml_dtypes.bfloat16).astype(np.float64), axis, -1)
    blocks = v.reshape(v.shape[:-1] + (-1, 32))
    amax = np.abs(blocks).max(-1, keepdims=True)
    byte = np.maximum(np.where(amax > 0, np.frexp(amax)[1] - 1 + 127, 0) - down, 1)
    scale = np.exp2(byte - 127.0)
    codes = (blocks / scale).astype(np.float32).astype(dtype).astype(np.float64)
    return np.moveaxis((codes * scale).reshape(v.shape), -1, axis)


WIDE = False


def mx_kscale(k, group=512):
    if not WIDE:
        return np.ones(k)
    levels = np.array([18, -18])
    if group != 512:
        return np.exp2(np.random.permutation(np.resize(levels, k // group))).repeat(group)
    if k % 512:
        return np.exp2(np.random.permutation(np.resize(levels, k // 32))).repeat(32)
    a = np.empty((k // 512, 16))
    for p in range(k // 512):
        a[p, :8] = np.random.permutation(np.resize(levels, 8))
        for g in range(8):
            far = levels[np.abs(levels - a[p, g]) >= 10]
            a[p, g + 8] = far[np.random.randint(len(far))]
    return np.exp2(a.ravel()).repeat(32)


def f64(x):
    return np.asarray(x).astype(np.float64)


def sigmoid(v):
    return 1.0 / (1.0 + np.exp(-v))


G, D, M, N = 4, 128, 128, 512


def setup_inputs():
    n = np.random.standard_normal
    s_d = mx_kscale(D, 0)
    return {
        "x": (n((G, D, N)) * s_d[:, None]).astype(np.float32),
        "w1": (n((G, D, M)) / np.sqrt(D) / s_d[:, None]).astype(np.float32),
        "w2": (n((G, D, M)) / np.sqrt(D) / s_d[:, None]).astype(np.float32),
        "w3": (n((G, D, M)) / np.sqrt(D) / s_d[:, None]).astype(np.float32),
        "th": (0.5 * n((G, M, 1))).astype(np.float32),
        "dx": (n((G, D, N)) * s_d[:, None]).astype(np.float32),
        "og": (np.random.uniform(0.5, 2.0, (G, M, 1))).astype(np.float32),
        "base": (0.3 * n((G, M, N))).astype(np.float32),
    }


def reference(x, w1, w2, w3, th, dx, og, base):
    w1q = mxq(f64(w1), 1, "e4m3")
    xq = mxq(f64(x), 1, "e4m3")
    z1 = w1q.transpose(0, 2, 1) @ xq
    dxq = mxq(f64(dx), 1, "e4m3")
    tz1 = w1q.transpose(0, 2, 1) @ dxq
    w2q = mxq(f64(w2), 1, "e4m3")
    z2 = w2q.transpose(0, 2, 1) @ xq
    tz2 = w2q.transpose(0, 2, 1) @ dxq
    w3q = mxq(f64(w3), 1, "e4m3")
    z3 = w3q.transpose(0, 2, 1) @ xq
    tz3 = w3q.transpose(0, 2, 1) @ dxq
    g2 = sigmoid(z2)
    g3 = sigmoid(z3 - f64(th))
    xg2 = tz2 * g2 * (1.0 - g2)
    xg3 = tz3 * g3 * (1.0 - g3)
    xh = (tz1 * g2 + xg2 * z1) * g3 + xg3 * z1 * g2
    y = xh * f64(og) + f64(base)
    return y

@@ -1,0 +1,229 @@
+from contextlib import ExitStack
+
+import concourse.mybir as mybir
+
+G, D, M, N = 4, 128, 128, 512
+FLOPS = 6 * 2 * G * D * M * N
+
+F32 = mybir.dt.float32
+BF16 = mybir.dt.bfloat16
+U32 = mybir.dt.uint32
+U8 = mybir.dt.uint8
+FP8X4 = mybir.dt.float8_e4m3fn_x4
+ALU = mybir.AluOpType
+ACT = mybir.ActivationFunctionType
+
+P = 128
+PACK = 4
+ROWS = D // PACK
+HALF = N // 2
+STEPS = 2 * G
+RUN = 4
+
+
+def tile_rows_tntwogates_kernel(tc, x, w1, w2, w3, th, dx, og, base, out):
+    nc = tc.nc
+    with ExitStack() as ctx:
+        sb = ctx.enter_context(tc.tile_pool(name="sb", bufs=1))
+        ps = ctx.enter_context(tc.psum_pool(name="ps", bufs=1))
+        ctx.enter_context(tc.manual_schedule())
+
+        def load_k_first(src, cols, name):
+            width = cols.stop - cols.start
+            raw = sb.tile([P, PACK, width], F32, name=name)
+            nc.sync.dma_start(out=raw[:], in_=src.rearrange("g (p j) n -> (g p) j n", j=PACK)[:, :, cols])
+            return raw
+
+        def interleave(copy, raw, name):
+            width = raw.shape[2]
+            grouped = sb.tile([P, width, PACK], BF16, name=name, align_bytes=64)
+            copy(
+                out=grouped[:].rearrange("p (c i) j -> p c j i", i=RUN),
+                in_=raw[:].rearrange("p j (c i) -> p c j i", i=RUN),
+            )
+            return grouped
+
+        def quantize(grouped, codes, scales):
+            nc.vector.quantize_mx(
+                out=codes.bitcast(FP8X4), scales=scales, in_=grouped[:].rearrange("p n j -> p (n j)")
+            )
+
+        halves = [slice(0, HALF), slice(HALF, N)]
+        z_cols, tz_cols = halves
+
+        rows = sb.tile([P, 2 * P], F32, name="rows", align_bytes=64)
+        nc.vector.memset(rows[:], 0.0)
+        for k, vec in enumerate((th, og)):
+            nc.scalar.dma_start(
+                out=rows[0:P:32, k * P : (k + 1) * P].rearrange("q (g i) -> q g i", g=G),
+                in_=vec.rearrange("g (q i) o -> q g (i o)", q=4),
+            )
+
+        x_raw = [load_k_first(x, halves[0], "x_raw0")]
+        dx_raw = [load_k_first(dx, halves[0], "dx_raw0")]
+        w_raw = {}
+        for k, w in ((2, w2), (3, w3), (1, w1)):
+            w_raw[k] = load_k_first(w, slice(0, M), "w_raw%d" % k)
+        x_raw.append(load_k_first(x, halves[1], "x_raw1"))
+        dx_raw.append(load_k_first(dx, halves[1], "dx_raw1"))
+        base_sb = []
+        for g in range(G):
+            t = sb.tile([P, N], F32, name="base%d" % g)
+            nc.sync.dma_start(out=t[:], in_=base[g])
+            base_sb.append(t)
+
+        a_codes = [sb.tile([P, N], U32, name="a_codes%d" % h, align_bytes=64) for h in range(2)]
+        a_scales = [sb.tile([P, N], U8, name="a_scales%d" % h, align_bytes=64) for h in range(2)]
+        w_codes = {k: sb.tile([P, M], U32, name="w_codes%d" % k, align_bytes=64) for k in (1, 2, 3)}
+        w_scales = {k: sb.tile([P, M], U8, name="w_scales%d" % k, align_bytes=64) for k in (1, 2, 3)}
+        banks = [[ps.tile([P, N], F32, name="bank%d_%d" % (g, i)) for i in range(2)] for g in range(G)]
+
+        def quantize_w(k, grouped):
+            quantize(grouped, w_codes[k][:], w_scales[k][:])
+
+        def quantize_a(h, cols, grouped):
+            quantize(grouped, a_codes[h][:, cols], a_scales[h][:, cols])
+
+        def bank(k, s):
+            h, g = divmod(s, G)
+            return banks[g][(h + (k == 3)) % 2]
+
+        def product(k, s):
+            h, g = divmod(s, G)
+            part = slice(ROWS * g, ROWS * (g + 1))
+            nc.tensor.matmul_mx(
+                out=bank(k, s)[:],
+                lhsT=w_codes[k][part, :].bitcast(FP8X4),
+                lhsT_scale=w_scales[k][part, :],
+                rhs=a_codes[h][part, :].bitcast(FP8X4),
+                rhs_scale=a_scales[h][part, :],
+                start=True,
+                stop=True,
+            )
+
+        vals = {}
+
+        def val(name, s):
+            if (name, s) not in vals:
+                vals[(name, s)] = sb.tile([P, HALF], F32, name="%s%d" % (name, s))
+            return vals[(name, s)]
+
+        x_bf = interleave(nc.vector.tensor_copy, x_raw[0], "x_bf0")
+        cols_t = sb.tile([P, 2 * P], F32, name="cols_t", align_bytes=64)
+        nc.vector.transpose(cols_t[:], rows[:])
+        quantize_a(0, z_cols, x_bf)
+        neg_th = sb.tile([P, G], F32, name="neg_th")
+        nc.vector.tensor_scalar(neg_th[:], cols_t[:, 0:P:32], -1.0, None, op0=ALU.mult)
+        dx_bf = interleave(nc.vector.tensor_copy, dx_raw[0], "dx_bf0")
+        w2_bf = interleave(nc.vector.tensor_copy, w_raw[2], "w_bf2")
+        quantize_a(0, tz_cols, dx_bf)
+        quantize_w(2, w2_bf)
+        w3_bf = interleave(nc.vector.tensor_copy, w_raw[3], "w_bf3")
+        w1_bf = interleave(nc.vector.tensor_copy, w_raw[1], "w_bf1")
+        quantize_w(3, w3_bf)
+        quantize_w(1, w1_bf)
+
+        def gate2(s):
+            nc.scalar.activation(val("g2", s)[:], bank(2, s)[:, z_cols], ACT.Sigmoid)
+
+        def gate3(s):
+            g = s % G
+            nc.scalar.activation(val("g3", s)[:], bank(3, s)[:, z_cols], ACT.Sigmoid, bias=neg_th[:, g : g + 1])
+
+        def op_a(s):
+            nc.vector.scalar_tensor_tensor(
+                val("a", s)[:], val("g2", s)[:], 1.0, bank(2, s)[:, tz_cols], op0=ALU.subtract, op1=ALU.mult
+            )
+
+        def op_b(s):
+            nc.vector.scalar_tensor_tensor(
+                val("b", s)[:], val("g3", s)[:], 1.0, bank(3, s)[:, tz_cols], op0=ALU.subtract, op1=ALU.mult
+            )
+
+        def op_c(s):
+            nc.vector.tensor_tensor(val("c", s)[:], val("a", s)[:], val("b", s)[:], op=ALU.add)
+
+        def op_gg(s):
+            nc.vector.tensor_tensor(val("gg", s)[:], val("g2", s)[:], val("g3", s)[:], op=ALU.mult)
+
+        def op_d(s, lo=0, hi=HALF):
+            nc.vector.tensor_tensor(val("d", s)[:, lo:hi], bank(1, s)[:, lo:hi], val("c", s)[:, lo:hi], op=ALU.mult)
+
+        def op_e(s, lo=0, hi=HALF):
+            nc.vector.tensor_tensor(
+                val("e", s)[:, lo:hi], bank(1, s)[:, HALF + lo : HALF + hi], val("d", s)[:, lo:hi], op=ALU.subtract
+            )
+
+        def op_f(s, lo=0, hi=HALF):
+            g = s % G
+            gain = cols_t[:, P + 32 * g : P + 32 * g + 1]
+            nc.vector.scalar_tensor_tensor(
+                val("f", s)[:, lo:hi], val("e", s)[:, lo:hi], gain, val("gg", s)[:, lo:hi], op0=ALU.mult, op1=ALU.mult
+            )
+
+        def op_y(s, lo=0, hi=HALF):
+            h, g = divmod(s, G)
+            nc.vector.tensor_tensor(
+                val("y", s)[:, lo:hi],
+                val("f", s)[:, lo:hi],
+                base_sb[g][:, h * HALF + lo : h * HALF + hi],
+                op=ALU.add,
+            )
+
+        def store(s):
+            h, g = divmod(s, G)
+            nc.sync.dma_start(out=out[g, :, halves[h]], in_=val("y", s)[:])
+
+        def prepare(s):
+            product(2, s)
+            product(3, s)
+            gate2(s)
+            gate3(s)
+
+        product(2, 0)
+        product(2, 1)
+        product(3, 0)
+        product(3, 1)
+        gate2(0)
+        gate2(1)
+        gate3(0)
+        gate3(1)
+        op_a(0)
+        prepare(2)
+        product(1, 0)
+        x1_bf = interleave(nc.scalar.copy, x_raw[1], "x_bf1")
+        op_a(1)
+        product(1, 1)
+        op_b(0)
+        op_gg(0)
+        op_c(0)
+        for t in range(1, STEPS):
+            if t == 1:
+                product(2, 3)
+                product(3, 3)
+                gate2(3)
+                dx1_bf = interleave(nc.scalar.copy, dx_raw[1], "dx_bf1")
+                gate3(3)
+            elif t + 2 < STEPS and t + 2 != G:
+                prepare(t + 2)
+            op_d(t - 1)
+            op_b(t)
+            op_e(t - 1)
+            if t + 1 < STEPS:
+                op_a(t + 1)
+                product(1, t + 1)
+            op_c(t)
+            op_f(t - 1)
+            if t == 1:
+                quantize_a(1, z_cols, x1_bf)
+            if t == 2:
+                quantize_a(1, tz_cols, dx1_bf)
+                prepare(G)
+            op_gg(t)
+            op_y(t - 1)
+            store(t - 1)
+        last = STEPS - 1
+        for op in (op_d, op_e, op_f, op_y):
+            op(last, 0, HALF // 2)
+            op(last, HALF // 2, HALF)
+        store(last)

@@ -36,7 +36,7 @@ def tile_rows_tntwogates_kernel(tc, x, w1, w2, w3, th, dx, og, base, out):
 
         def interleave(copy, raw, name):
             width = raw.shape[2]
-            grouped = sb.tile([P, width, PACK], BF16, name=name, align_bytes=64)
+            grouped = sb.tile([P, width, PACK], BF16, name=name, tag=name, align_bytes=64)
             copy(
                 out=grouped[:].rearrange("p (c i) j -> p c j i", i=RUN),
                 in_=raw[:].rearrange("p j (c i) -> p c j i", i=RUN),
@@ -53,23 +53,23 @@ def tile_rows_tntwogates_kernel(tc, x, w1, w2, w3, th, dx, og, base, out):
 
         rows = sb.tile([P, 2 * P], F32, name="rows", align_bytes=64)
         nc.vector.memset(rows[:], 0.0)
-        for k, vec in enumerate((th, og)):
-            nc.scalar.dma_start(
-                out=rows[0:P:32, k * P : (k + 1) * P].rearrange("q (g i) -> q g i", g=G),
-                in_=vec.rearrange("g (q i) o -> q g (i o)", q=4),
-            )
-
         x_raw = [load_k_first(x, halves[0], "x_raw0")]
         dx_raw = [load_k_first(dx, halves[0], "dx_raw0")]
         w_raw = {}
-        for k, w in ((2, w2), (3, w3), (1, w1)):
+        for k, w in ((2, w2), (3, w3)):
             w_raw[k] = load_k_first(w, slice(0, M), "w_raw%d" % k)
+        for k, vec in enumerate((th, og)):
+            nc.sync.dma_start(
+                out=rows[0:P:32, k * P : (k + 1) * P].rearrange("q (g i) -> q g i", g=G),
+                in_=vec.rearrange("g (q i) o -> q g (i o)", q=4),
+            )
         x_raw.append(load_k_first(x, halves[1], "x_raw1"))
+        w_raw[1] = load_k_first(w1, slice(0, M), "w_raw1")
         dx_raw.append(load_k_first(dx, halves[1], "dx_raw1"))
         base_sb = []
-        for g in range(G):
-            t = sb.tile([P, N], F32, name="base%d" % g)
-            nc.sync.dma_start(out=t[:], in_=base[g])
+        for u in range(G // 2):
+            t = sb.tile([P, 2, N], F32, name="base%d" % u)
+            nc.sync.dma_start(out=t[:], in_=base[2 * u : 2 * u + 2].rearrange("g m n -> m g n"))
             base_sb.append(t)
 
         a_codes = [sb.tile([P, N], U32, name="a_codes%d" % h, align_bytes=64) for h in range(2)]
@@ -103,48 +103,53 @@ def tile_rows_tntwogates_kernel(tc, x, w1, w2, w3, th, dx, og, base, out):
 
         vals = {}
 
+        def pair(name, r):
+            if (name, r) not in vals:
+                vals[(name, r)] = sb.tile([P, 2 * HALF], F32, name="%s%d" % (name, r))
+            return vals[(name, r)]
+
         def val(name, s):
-            if (name, s) not in vals:
-                vals[(name, s)] = sb.tile([P, HALF], F32, name="%s%d" % (name, s))
-            return vals[(name, s)]
+            if name in ("a", "b"):
+                return pair("ab", s)[:, (name == "b") * HALF : ((name == "b") + 1) * HALF]
+            return pair(name, s // 2)[:, (s % 2) * HALF : (s % 2 + 1) * HALF]
 
         x_bf = interleave(nc.vector.tensor_copy, x_raw[0], "x_bf0")
-        cols_t = sb.tile([P, 2 * P], F32, name="cols_t", align_bytes=64)
-        nc.vector.transpose(cols_t[:], rows[:])
         quantize_a(0, z_cols, x_bf)
-        neg_th = sb.tile([P, G], F32, name="neg_th")
-        nc.vector.tensor_scalar(neg_th[:], cols_t[:, 0:P:32], -1.0, None, op0=ALU.mult)
         dx_bf = interleave(nc.vector.tensor_copy, dx_raw[0], "dx_bf0")
         w2_bf = interleave(nc.vector.tensor_copy, w_raw[2], "w_bf2")
         quantize_a(0, tz_cols, dx_bf)
         quantize_w(2, w2_bf)
         w3_bf = interleave(nc.vector.tensor_copy, w_raw[3], "w_bf3")
-        w1_bf = interleave(nc.vector.tensor_copy, w_raw[1], "w_bf1")
+        cols_t = sb.tile([P, 2 * P], F32, name="cols_t", align_bytes=64)
+        nc.vector.transpose(cols_t[:], rows[:])
         quantize_w(3, w3_bf)
-        quantize_w(1, w1_bf)
+        neg_th = sb.tile([P, G], F32, name="neg_th")
+        nc.vector.tensor_scalar(neg_th[:], cols_t[:, 0:P:32], -1.0, None, op0=ALU.mult)
+        x1_bf = interleave(nc.vector.tensor_copy, x_raw[1], "x_bf1")
+        w1_bf = interleave(nc.vector.tensor_copy, w_raw[1], "w_bf1")
 
         def gate2(s):
-            nc.scalar.activation(val("g2", s)[:], bank(2, s)[:, z_cols], ACT.Sigmoid)
+            nc.scalar.activation(val("g2", s), bank(2, s)[:, z_cols], ACT.Sigmoid)
 
         def gate3(s):
             g = s % G
-            nc.scalar.activation(val("g3", s)[:], bank(3, s)[:, z_cols], ACT.Sigmoid, bias=neg_th[:, g : g + 1])
+            nc.scalar.activation(val("g3", s), bank(3, s)[:, z_cols], ACT.Sigmoid, bias=neg_th[:, g : g + 1])
 
         def op_a(s):
             nc.vector.scalar_tensor_tensor(
-                val("a", s)[:], val("g2", s)[:], 1.0, bank(2, s)[:, tz_cols], op0=ALU.subtract, op1=ALU.mult
+                val("a", s), val("g2", s), 1.0, bank(2, s)[:, tz_cols], op0=ALU.subtract, op1=ALU.mult
             )
 
         def op_b(s):
             nc.vector.scalar_tensor_tensor(
-                val("b", s)[:], val("g3", s)[:], 1.0, bank(3, s)[:, tz_cols], op0=ALU.subtract, op1=ALU.mult
+                val("b", s), val("g3", s), 1.0, bank(3, s)[:, tz_cols], op0=ALU.subtract, op1=ALU.mult
             )
 
         def op_c(s):
-            nc.vector.tensor_tensor(val("c", s)[:], val("a", s)[:], val("b", s)[:], op=ALU.add)
+            nc.vector.tensor_tensor(val("c", s), val("a", s), val("b", s), op=ALU.add)
 
-        def op_gg(s):
-            nc.vector.tensor_tensor(val("gg", s)[:], val("g2", s)[:], val("g3", s)[:], op=ALU.mult)
+        def op_gg(r):
+            nc.gpsimd.tensor_tensor(pair("gg", r)[:], pair("g2", r)[:], pair("g3", r)[:], op=ALU.mult)
 
         def op_d(s, lo=0, hi=HALF):
             nc.vector.tensor_tensor(val("d", s)[:, lo:hi], bank(1, s)[:, lo:hi], val("c", s)[:, lo:hi], op=ALU.mult)
@@ -161,69 +166,79 @@ def tile_rows_tntwogates_kernel(tc, x, w1, w2, w3, th, dx, og, base, out):
                 val("f", s)[:, lo:hi], val("e", s)[:, lo:hi], gain, val("gg", s)[:, lo:hi], op0=ALU.mult, op1=ALU.mult
             )
 
-        def op_y(s, lo=0, hi=HALF):
+        def op_y_pair(r):
+            h, u = divmod(r, G // 2)
+            y = pair("y", r)[:].rearrange("p (g n) -> p g n", g=2)
+            f = pair("f", r)[:].rearrange("p (g n) -> p g n", g=2)
+            nc.gpsimd.tensor_tensor(y, f, base_sb[u][:, :, halves[h]], op=ALU.add)
+            nc.sync.dma_start(out=out[2 * u : 2 * u + 2, :, halves[h]].rearrange("g m n -> m g n"), in_=y)
+
+        def op_y(s, lo, hi, queue):
             h, g = divmod(s, G)
+            cols = slice(h * HALF + lo, h * HALF + hi)
             nc.vector.tensor_tensor(
-                val("y", s)[:, lo:hi],
-                val("f", s)[:, lo:hi],
-                base_sb[g][:, h * HALF + lo : h * HALF + hi],
-                op=ALU.add,
+                val("y", s)[:, lo:hi], val("f", s)[:, lo:hi], base_sb[g // 2][:, g % 2, cols], op=ALU.add
             )
+            queue.dma_start(out=out[g, :, cols], in_=val("y", s)[:, lo:hi])
 
-        def store(s):
-            h, g = divmod(s, G)
-            nc.sync.dma_start(out=out[g, :, halves[h]], in_=val("y", s)[:])
+        def both(op, r):
+            op(2 * r)
+            op(2 * r + 1)
 
-        def prepare(s):
-            product(2, s)
-            product(3, s)
-            gate2(s)
-            gate3(s)
+        def products(k, r):
+            product(k, 2 * r)
+            product(k, 2 * r + 1)
 
-        product(2, 0)
-        product(2, 1)
-        product(3, 0)
-        product(3, 1)
-        gate2(0)
-        gate2(1)
-        gate3(0)
-        gate3(1)
+        products(2, 0)
+        products(3, 0)
+        both(gate2, 0)
+        both(gate3, 0)
+        products(2, 1)
+        products(3, 1)
+        both(gate2, 1)
         op_a(0)
-        prepare(2)
-        product(1, 0)
-        x1_bf = interleave(nc.scalar.copy, x_raw[1], "x_bf1")
+        quantize_w(1, w1_bf)
         op_a(1)
-        product(1, 1)
-        op_b(0)
-        op_gg(0)
-        op_c(0)
-        for t in range(1, STEPS):
-            if t == 1:
-                product(2, 3)
-                product(3, 3)
-                gate2(3)
-                dx1_bf = interleave(nc.scalar.copy, dx_raw[1], "dx_bf1")
-                gate3(3)
-            elif t + 2 < STEPS and t + 2 != G:
-                prepare(t + 2)
-            op_d(t - 1)
-            op_b(t)
-            op_e(t - 1)
-            if t + 1 < STEPS:
-                op_a(t + 1)
-                product(1, t + 1)
-            op_c(t)
-            op_f(t - 1)
-            if t == 1:
-                quantize_a(1, z_cols, x1_bf)
-            if t == 2:
+        products(1, 0)
+        quantize_a(1, z_cols, x1_bf)
+        dx1_bf = interleave(nc.scalar.copy, dx_raw[1], "dx_bf1")
+        both(gate3, 1)
+        both(op_b, 0)
+        both(op_c, 0)
+        vals[("gg", 0)] = pair("ab", 0)
+        rounds = STEPS // 2
+        for r in range(1, rounds):
+            if r == 1:
+                op_gg(0)
+            else:
+                op_y_pair(r - 2)
+                op_gg(r)
+            both(op_d, r - 1)
+            both(op_e, r - 1)
+            if r == 1:
                 quantize_a(1, tz_cols, dx1_bf)
-                prepare(G)
-            op_gg(t)
-            op_y(t - 1)
-            store(t - 1)
-        last = STEPS - 1
-        for op in (op_d, op_e, op_f, op_y):
-            op(last, 0, HALF // 2)
-            op(last, HALF // 2, HALF)
-        store(last)
+                vals[("gg", 1)] = sb.tile([P, 2 * HALF], F32, name="gg1", tag="dx_bf1", align_bytes=64)
+                op_gg(1)
+                products(2, 2)
+                products(3, 2)
+                both(gate2, 2)
+                both(gate3, 2)
+            if r == 2:
+                products(3, 3)
+                both(gate3, 3)
+            both(op_a, r)
+            products(1, r)
+            both(op_b, r)
+            if r == 1:
+                products(2, 3)
+                both(gate2, 3)
+            op_f(2 * r - 2)
+            op_c(2 * r)
+            op_f(2 * r - 1)
+            op_c(2 * r + 1)
+        op_y_pair(rounds - 2)
+        both(op_d, rounds - 1)
+        both(op_e, rounds - 1)
+        both(op_f, rounds - 1)
+        op_y(STEPS - 2, 0, HALF, nc.sync)
+        op_y(STEPS - 1, 0, HALF, nc.sync)

@@ -200,10 +200,10 @@ def tile_rows_tntwogates_kernel(tc, x, w1, w2, w3, th, dx, og, base, out):
         quantize_w(1, w1_bf)
         op_a(1)
         products(1, 0)
-        quantize_a(1, z_cols, x1_bf)
         dx1_bf = interleave(nc.scalar.copy, dx_raw[1], "dx_bf1")
         both(gate3, 1)
         both(op_b, 0)
+        quantize_a(1, z_cols, x1_bf)
         both(op_c, 0)
         vals[("gg", 0)] = pair("ab", 0)
         rounds = STEPS // 2
@@ -213,22 +213,22 @@ def tile_rows_tntwogates_kernel(tc, x, w1, w2, w3, th, dx, og, base, out):
             else:
                 op_y_pair(r - 2)
                 op_gg(r)
-            both(op_d, r - 1)
-            both(op_e, r - 1)
+            for i in range(2):
+                op_a(2 * r + i)
+                product(1, 2 * r + i)
+                op_d(2 * r - 2 + i)
             if r == 1:
                 quantize_a(1, tz_cols, dx1_bf)
                 vals[("gg", 1)] = sb.tile([P, 2 * HALF], F32, name="gg1", tag="dx_bf1", align_bytes=64)
                 op_gg(1)
                 products(2, 2)
-                products(3, 2)
                 both(gate2, 2)
-                both(gate3, 2)
-            if r == 2:
-                products(3, 3)
-                both(gate3, 3)
-            both(op_a, r)
-            products(1, r)
-            both(op_b, r)
+            for i in range(2):
+                op_b(2 * r + i)
+                op_e(2 * r - 2 + i)
+                if r + 1 < rounds:
+                    product(3, 2 * r + 2 + i)
+                    gate3(2 * r + 2 + i)
             if r == 1:
                 products(2, 3)
                 both(gate2, 3)

@@ -18,7 +18,7 @@ PACK = 4
 ROWS = D // PACK
 HALF = N // 2
 STEPS = 2 * G
-RUN = 4
+RUN = 2
 
 
 def tile_rows_tntwogates_kernel(tc, x, w1, w2, w3, th, dx, og, base, out):

from contextlib import ExitStack

import concourse.mybir as mybir

G, D, M, N = 4, 128, 128, 512
FLOPS = 6 * 2 * G * D * M * N

F32 = mybir.dt.float32
BF16 = mybir.dt.bfloat16
U32 = mybir.dt.uint32
U8 = mybir.dt.uint8
FP8X4 = mybir.dt.float8_e4m3fn_x4
ALU = mybir.AluOpType
ACT = mybir.ActivationFunctionType

P = 128
PACK = 4
ROWS = D // PACK
HALF = N // 2
STEPS = 2 * G
RUN = 2


def tile_rows_tntwogates_kernel(tc, x, w1, w2, w3, th, dx, og, base, out):
    nc = tc.nc
    with ExitStack() as ctx:
        sb = ctx.enter_context(tc.tile_pool(name="sb", bufs=1))
        ps = ctx.enter_context(tc.psum_pool(name="ps", bufs=1))
        ctx.enter_context(tc.manual_schedule())

        def load_k_first(src, cols, name):
            width = cols.stop - cols.start
            raw = sb.tile([P, PACK, width], F32, name=name)
            nc.sync.dma_start(out=raw[:], in_=src.rearrange("g (p j) n -> (g p) j n", j=PACK)[:, :, cols])
            return raw

        def interleave(copy, raw, name):
            width = raw.shape[2]
            grouped = sb.tile([P, width, PACK], BF16, name=name, tag=name, align_bytes=64)
            copy(
                out=grouped[:].rearrange("p (c i) j -> p c j i", i=RUN),
                in_=raw[:].rearrange("p j (c i) -> p c j i", i=RUN),
            )
            return grouped

        def quantize(grouped, codes, scales):
            nc.vector.quantize_mx(
                out=codes.bitcast(FP8X4), scales=scales, in_=grouped[:].rearrange("p n j -> p (n j)")
            )

        halves = [slice(0, HALF), slice(HALF, N)]
        z_cols, tz_cols = halves

        rows = sb.tile([P, 2 * P], F32, name="rows", align_bytes=64)
        nc.vector.memset(rows[:], 0.0)
        x_raw = [load_k_first(x, halves[0], "x_raw0")]
        dx_raw = [load_k_first(dx, halves[0], "dx_raw0")]
        w_raw = {}
        for k, w in ((2, w2), (3, w3)):
            w_raw[k] = load_k_first(w, slice(0, M), "w_raw%d" % k)
        for k, vec in enumerate((th, og)):
            nc.sync.dma_start(
                out=rows[0:P:32, k * P : (k + 1) * P].rearrange("q (g i) -> q g i", g=G),
                in_=vec.rearrange("g (q i) o -> q g (i o)", q=4),
            )
        x_raw.append(load_k_first(x, halves[1], "x_raw1"))
        w_raw[1] = load_k_first(w1, slice(0, M), "w_raw1")
        dx_raw.append(load_k_first(dx, halves[1], "dx_raw1"))
        base_sb = []
        for u in range(G // 2):
            t = sb.tile([P, 2, N], F32, name="base%d" % u)
            nc.sync.dma_start(out=t[:], in_=base[2 * u : 2 * u + 2].rearrange("g m n -> m g n"))
            base_sb.append(t)

        a_codes = [sb.tile([P, N], U32, name="a_codes%d" % h, align_bytes=64) for h in range(2)]
        a_scales = [sb.tile([P, N], U8, name="a_scales%d" % h, align_bytes=64) for h in range(2)]
        w_codes = {k: sb.tile([P, M], U32, name="w_codes%d" % k, align_bytes=64) for k in (1, 2, 3)}
        w_scales = {k: sb.tile([P, M], U8, name="w_scales%d" % k, align_bytes=64) for k in (1, 2, 3)}
        banks = [[ps.tile([P, N], F32, name="bank%d_%d" % (g, i)) for i in range(2)] for g in range(G)]

        def quantize_w(k, grouped):
            quantize(grouped, w_codes[k][:], w_scales[k][:])

        def quantize_a(h, cols, grouped):
            quantize(grouped, a_codes[h][:, cols], a_scales[h][:, cols])

        def bank(k, s):
            h, g = divmod(s, G)
            return banks[g][(h + (k == 3)) % 2]

        def product(k, s):
            h, g = divmod(s, G)
            part = slice(ROWS * g, ROWS * (g + 1))
            nc.tensor.matmul_mx(
                out=bank(k, s)[:],
                lhsT=w_codes[k][part, :].bitcast(FP8X4),
                lhsT_scale=w_scales[k][part, :],
                rhs=a_codes[h][part, :].bitcast(FP8X4),
                rhs_scale=a_scales[h][part, :],
                start=True,
                stop=True,
            )

        vals = {}

        def pair(name, r):
            if (name, r) not in vals:
                vals[(name, r)] = sb.tile([P, 2 * HALF], F32, name="%s%d" % (name, r))
            return vals[(name, r)]

        def val(name, s):
            if name in ("a", "b"):
                return pair("ab", s)[:, (name == "b") * HALF : ((name == "b") + 1) * HALF]
            return pair(name, s // 2)[:, (s % 2) * HALF : (s % 2 + 1) * HALF]

        x_bf = interleave(nc.vector.tensor_copy, x_raw[0], "x_bf0")
        quantize_a(0, z_cols, x_bf)
        dx_bf = interleave(nc.vector.tensor_copy, dx_raw[0], "dx_bf0")
        w2_bf = interleave(nc.vector.tensor_copy, w_raw[2], "w_bf2")
        quantize_a(0, tz_cols, dx_bf)
        quantize_w(2, w2_bf)
        w3_bf = interleave(nc.vector.tensor_copy, w_raw[3], "w_bf3")
        cols_t = sb.tile([P, 2 * P], F32, name="cols_t", align_bytes=64)
        nc.vector.transpose(cols_t[:], rows[:])
        quantize_w(3, w3_bf)
        neg_th = sb.tile([P, G], F32, name="neg_th")
        nc.vector.tensor_scalar(neg_th[:], cols_t[:, 0:P:32], -1.0, None, op0=ALU.mult)
        x1_bf = interleave(nc.vector.tensor_copy, x_raw[1], "x_bf1")
        w1_bf = interleave(nc.vector.tensor_copy, w_raw[1], "w_bf1")

        def gate2(s):
            nc.scalar.activation(val("g2", s), bank(2, s)[:, z_cols], ACT.Sigmoid)

        def gate3(s):
            g = s % G
            nc.scalar.activation(val("g3", s), bank(3, s)[:, z_cols], ACT.Sigmoid, bias=neg_th[:, g : g + 1])

        def op_a(s):
            nc.vector.scalar_tensor_tensor(
                val("a", s), val("g2", s), 1.0, bank(2, s)[:, tz_cols], op0=ALU.subtract, op1=ALU.mult
            )

        def op_b(s):
            nc.vector.scalar_tensor_tensor(
                val("b", s), val("g3", s), 1.0, bank(3, s)[:, tz_cols], op0=ALU.subtract, op1=ALU.mult
            )

        def op_c(s):
            nc.vector.tensor_tensor(val("c", s), val("a", s), val("b", s), op=ALU.add)

        def op_gg(r):
            nc.gpsimd.tensor_tensor(pair("gg", r)[:], pair("g2", r)[:], pair("g3", r)[:], op=ALU.mult)

        def op_d(s, lo=0, hi=HALF):
            nc.vector.tensor_tensor(val("d", s)[:, lo:hi], bank(1, s)[:, lo:hi], val("c", s)[:, lo:hi], op=ALU.mult)

        def op_e(s, lo=0, hi=HALF):
            nc.vector.tensor_tensor(
                val("e", s)[:, lo:hi], bank(1, s)[:, HALF + lo : HALF + hi], val("d", s)[:, lo:hi], op=ALU.subtract
            )

        def op_f(s, lo=0, hi=HALF):
            g = s % G
            gain = cols_t[:, P + 32 * g : P + 32 * g + 1]
            nc.vector.scalar_tensor_tensor(
                val("f", s)[:, lo:hi], val("e", s)[:, lo:hi], gain, val("gg", s)[:, lo:hi], op0=ALU.mult, op1=ALU.mult
            )

        def op_y_pair(r):
            h, u = divmod(r, G // 2)
            y = pair("y", r)[:].rearrange("p (g n) -> p g n", g=2)
            f = pair("f", r)[:].rearrange("p (g n) -> p g n", g=2)
            nc.gpsimd.tensor_tensor(y, f, base_sb[u][:, :, halves[h]], op=ALU.add)
            nc.sync.dma_start(out=out[2 * u : 2 * u + 2, :, halves[h]].rearrange("g m n -> m g n"), in_=y)

        def op_y(s, lo, hi, queue):
            h, g = divmod(s, G)
            cols = slice(h * HALF + lo, h * HALF + hi)
            nc.vector.tensor_tensor(
                val("y", s)[:, lo:hi], val("f", s)[:, lo:hi], base_sb[g // 2][:, g % 2, cols], op=ALU.add
            )
            queue.dma_start(out=out[g, :, cols], in_=val("y", s)[:, lo:hi])

        def both(op, r):
            op(2 * r)
            op(2 * r + 1)

        def products(k, r):
            product(k, 2 * r)
            product(k, 2 * r + 1)

        products(2, 0)
        products(3, 0)
        both(gate2, 0)
        both(gate3, 0)
        products(2, 1)
        products(3, 1)
        both(gate2, 1)
        op_a(0)
        quantize_w(1, w1_bf)
        op_a(1)
        products(1, 0)
        dx1_bf = interleave(nc.scalar.copy, dx_raw[1], "dx_bf1")
        both(gate3, 1)
        both(op_b, 0)
        quantize_a(1, z_cols, x1_bf)
        both(op_c, 0)
        vals[("gg", 0)] = pair("ab", 0)
        rounds = STEPS // 2
        for r in range(1, rounds):
            if r == 1:
                op_gg(0)
            else:
                op_y_pair(r - 2)
                op_gg(r)
            for i in range(2):
                op_a(2 * r + i)
                product(1, 2 * r + i)
                op_d(2 * r - 2 + i)
            if r == 1:
                quantize_a(1, tz_cols, dx1_bf)
                vals[("gg", 1)] = sb.tile([P, 2 * HALF], F32, name="gg1", tag="dx_bf1", align_bytes=64)
                op_gg(1)
                products(2, 2)
                both(gate2, 2)
            for i in range(2):
                op_b(2 * r + i)
                op_e(2 * r - 2 + i)
                if r + 1 < rounds:
                    product(3, 2 * r + 2 + i)
                    gate3(2 * r + 2 + i)
            if r == 1:
                products(2, 3)
                both(gate2, 3)
            op_f(2 * r - 2)
            op_c(2 * r)
            op_f(2 * r - 1)
            op_c(2 * r + 1)
        op_y_pair(rounds - 2)
        both(op_d, rounds - 1)
        both(op_e, rounds - 1)
        both(op_f, rounds - 1)
        op_y(STEPS - 2, 0, HALF, nc.sync)
        op_y(STEPS - 1, 0, HALF, nc.sync)
